import numpy as np
import ml_dtypes


def mxq(x, axis, fmt="e4m3"):
    dtype, down = {"e4m3": (ml_dtypes.float8_e4m3fn, 7), "e5m2": (ml_dtypes.float8_e5m2, 14)}[fmt]
    v = np.moveaxis(np.asarray(x, np.float32).astype(ml_dtypes.bfloat16).astype(np.float64), axis, -1)
    blocks = v.reshape(v.shape[:-1] + (-1, 32))
    amax = np.abs(blocks).max(-1, keepdims=True)
    byte = np.maximum(np.where(amax > 0, np.frexp(amax)[1] - 1 + 127, 0) - down, 1)
    scale = np.exp2(byte - 127.0)
    codes = (blocks / scale).astype(np.float32).astype(dtype).astype(np.float64)
    return np.moveaxis((codes * scale).reshape(v.shape), -1, axis)


WIDE = False


def mx_kscale(k):
    if not WIDE:
        return np.ones(k)
    levels = np.array([10, -10, 5, -5, 0])
    if k % 512:
        return np.exp2(np.random.permutation(np.resize(levels, k // 32))).repeat(32)
    a = np.empty((k // 512, 16))
    for p in range(k // 512):
        a[p, :8] = np.random.permutation(np.resize(levels, 8))
        for g in range(8):
            far = levels[np.abs(levels - a[p, g]) >= 10]
            a[p, g + 8] = far[np.random.randint(len(far))]
    return np.exp2(a.ravel()).repeat(32)


def f64(x):
    return np.asarray(x).astype(np.float64)


def striped(idx):
    return np.tile(np.asarray(idx).reshape(-1, 16).T, (8, 1)).astype(np.uint16)


def unstriped(offs):
    return offs[:16].T.reshape(-1).astype(np.int64)


def striped8(idx):
    return np.asarray(idx).reshape(8, -1, 16).transpose(0, 2, 1).reshape(128, -1).astype(np.uint16)


def unstriped8(offs):
    return offs.reshape(8, 16, -1).transpose(0, 2, 1).reshape(8, -1).astype(np.int64)


def pick8(x, idx, run):
    r = np.arange(len(x))
    return x[r[:, None], idx[r % (8 * run) // run]]


E2M1 = np.array([0.0, 0.5, 1.0, 1.5, 2.0, 3.0, 4.0, 6.0, -0.0, -0.5, -1.0, -1.5, -2.0, -3.0, -4.0, -6.0])


def pack_weight(w, fmt):
    k, n = w.shape
    w = f64(np.asarray(w, np.float32).astype(ml_dtypes.bfloat16)).reshape(k // 32, 32, n)
    amax = np.abs(w).max(1)
    if fmt == "e4m3":
        byte = np.frexp(amax)[1] - 1 + 127 - 7
    else:
        mant, ex = np.frexp(amax / 6.0)
        byte = np.where(mant > 0.5, ex, ex - 1) + 127
    byte = np.clip(np.where(amax > 0, byte, 1), 1, 254)
    scaled = (w * np.exp2(127.0 - byte)[:, None, :]).reshape(k, n).astype(np.float32)
    by_word = np.ascontiguousarray(scaled.reshape(k // 512, 128, 4, n).transpose(0, 1, 3, 2))
    if fmt == "e4m3":
        words = by_word.astype(ml_dtypes.float8_e4m3fn).view(np.uint8)
    else:
        c = by_word.astype(ml_dtypes.float4_e2m1fn).view(np.uint8) & 0xF
        words = (c[..., 0::2] | (c[..., 1::2] << 4)).reshape(k // 512, 128, 2 * n)
    return np.ascontiguousarray(words), np.ascontiguousarray(byte.astype(np.uint8).reshape(k // 512, 16, n))


def unpack_weight(words, scales, fmt):
    g, _, n = scales.shape
    words = np.ascontiguousarray(words).reshape(g, 128, n, -1)
    if fmt == "e4m3":
        vals = words.view(ml_dtypes.float8_e4m3fn).astype(np.float64)
    else:
        nib = np.empty((g, 128, n, 4), np.uint8)
        nib[..., 0::2] = words & 0xF
        nib[..., 1::2] = words >> 4
        vals = E2M1[nib]
    vals = vals * np.repeat(np.exp2(scales.astype(np.float64) - 127.0), 8, axis=1)[..., None]
    return vals.transpose(0, 1, 3, 2).reshape(g * 512, n)


K, J, R, T, Z, M, O, N, U = 512, 256, 512, 1024, 512, 1024, 128, 256, 256


def setup_inputs():
    n = np.random.standard_normal
    idx = np.random.permutation(T)[:J]
    idx2 = np.random.permutation(M)[:J]
    idx3 = np.stack([np.random.permutation(J)[:O] for _ in range(8)])
    idx4 = np.stack([np.random.permutation(J)[:O] for _ in range(8)])
    idx5 = np.stack([np.random.permutation(U)[:O] for _ in range(8)])
    idx6 = np.stack([np.random.permutation(U)[:O] for _ in range(8)])
    fk = mx_kscale(K)
    fr = mx_kscale(R)
    fz = mx_kscale(Z)
    xtp = pack_weight(n((K, T)) * fk[:, None], "e4m3")
    wp = pack_weight(n((K, R)) * 1 / np.sqrt(K) / fk[:, None] * fr, "e4m3")
    xop = pack_weight(n((Z, M)) / fz[:, None], "e4m3")
    w2p = pack_weight(n((Z, R)) * 1 / np.sqrt(Z) * fz[:, None] * fr, "e2m1")
    wbp = pack_weight(n((R, N)) * 1 / np.sqrt(R) / fr[:, None], "e2m1")
    wop = pack_weight(n((R, N)) * 1 / np.sqrt(R) / fr[:, None], "e4m3")
    return {
        "xt_words": xtp[0],
        "xt_scales": xtp[1],
        "w_words": wp[0],
        "w_scales": wp[1],
        "xo_words": xop[0],
        "xo_scales": xop[1],
        "w2_words": w2p[0],
        "w2_scales": w2p[1],
        "sa": (np.random.uniform(0.5, 1.6, (R, 1))).astype(np.float32),
        "sb": (np.random.uniform(0.5, 1.6, (R, 1))).astype(np.float32),
        "wb_words": wbp[0],
        "wb_scales": wbp[1],
        "wo_words": wop[0],
        "wo_scales": wop[1],
        "offs": striped(idx),
        "offs2": striped(idx2),
        "offs3": striped8(idx3),
        "offs4": striped8(idx4),
        "offs5": striped8(idx5),
        "offs6": striped8(idx6),
    }


def reference(xt_words, xt_scales, w_words, w_scales, xo_words, xo_scales, w2_words, w2_scales, sa, sb, wb_words, wb_scales, wo_words, wo_scales, offs, offs2, offs3, offs4, offs5, offs6):
    idx = unstriped(offs)
    idx2 = unstriped(offs2)
    idx3 = unstriped8(offs3)
    idx4 = unstriped8(offs4)
    idx5 = unstriped8(offs5)
    idx6 = unstriped8(offs6)
    xtu = unpack_weight(xt_words, xt_scales, "e4m3")
    wu = unpack_weight(w_words, w_scales, "e4m3")
    xou = unpack_weight(xo_words, xo_scales, "e4m3")
    w2u = unpack_weight(w2_words, w2_scales, "e2m1")
    wbu = unpack_weight(wb_words, wb_scales, "e2m1")
    wou = unpack_weight(wo_words, wo_scales, "e4m3")
    xtidxg = xtu[:, idx]
    xoidx2g = xou[:, idx2]
    a = wu.T @ xtidxg + w2u.T @ xoidx2g
    hid = np.abs(pick8(a, idx3, 64) * f64(sa) - pick8(a, idx4, 64) * f64(sb))
    hidq = mxq(hid, 0, "e4m3")
    p = wbu.T @ hidq
    q = wou.T @ hidq
    m0 = np.zeros((N, U))
    m0[np.arange(N)[:, None], idx5[np.arange(N) % 128 // 16]] = p
    m1 = np.zeros((N, U))
    m1[np.arange(N)[:, None], idx6[np.arange(N) % 128 // 16]] = q
    y = m0 + m1
    return y

@@ -1,0 +1,167 @@
+from contextlib import ExitStack
+
+import concourse.mybir as mybir
+
+F32 = mybir.dt.float32
+BF16 = mybir.dt.bfloat16
+I32 = mybir.dt.int32
+U32 = mybir.dt.uint32
+U16 = mybir.dt.uint16
+U8 = mybir.dt.uint8
+FP8X4 = mybir.dt.float8_e4m3fn_x4
+FP4X4 = mybir.dt.float4_e2m1fn_x4
+ACT = mybir.ActivationFunctionType
+ALU = mybir.AluOpType
+
+P = 128
+K, J, R, T, Z, M, O, N, U = 512, 256, 512, 1024, 512, 1024, 128, 256, 256
+PACK = 4
+QUADS = 4
+HALF = O // 2
+FLOPS = 2 * (K * R * J + Z * R * J + 2 * R * N * O)
+
+
+def tile_picked_tokens_plain_bank_grouppair_outcomes_twoposted_kernel(
+    tc, xt_words, xt_scales, w_words, w_scales, xo_words, xo_scales, w2_words, w2_scales, sa, sb,
+    wb_words, wb_scales, wo_words, wo_scales, offs, offs2, offs3, offs4, offs5, offs6, out,
+):
+    nc = tc.nc
+    with ExitStack() as ctx:
+        lists = ctx.enter_context(tc.tile_pool(name="lists", bufs=1))
+        keep = ctx.enter_context(tc.tile_pool(name="keep", bufs=1))
+        ring = ctx.enter_context(tc.tile_pool(name="ring", bufs=1))
+        psum = ctx.enter_context(tc.psum_pool(name="psum", bufs=1))
+
+        def sb_tile(name, shape, dtype):
+            return keep.tile(shape, dtype, name=name, align_bytes=64)
+
+        def load_list(name, src):
+            t = lists.tile(list(src.shape), U16, name=name)
+            nc.sync.dma_start(t[:], src)
+            return t
+
+        def by_quadrant(scales):
+            return scales[0].rearrange("(q i) n -> i q n", i=PACK).bitcast(I32)
+
+        def words_of(words):
+            return words[0].rearrange("p n r -> p (n r)").bitcast(I32)
+
+        wsc_stage = sb_tile("wsc_stage", [32, QUADS, R // 4], I32)
+        nc.vector.memset(wsc_stage[:], 0)
+        xt_swin = sb_tile("xt_swin", [P, T], U8)
+        xo_swin = sb_tile("xo_swin", [P, M], U8)
+        nc.vector.memset(xt_swin[:].bitcast(I32), 0)
+        nc.vector.memset(xo_swin[:].bitcast(I32), 0)
+        wb_sc = sb_tile("wb_sc", [P, N], U8)
+        wo_sc = sb_tile("wo_sc", [P, N], U8)
+        nc.vector.memset(wb_sc[:].bitcast(I32), 0)
+        nc.vector.memset(wo_sc[:].bitcast(I32), 0)
+        hq = sb_tile("hq", [P, O], I32)
+        hs = sb_tile("hs", [P, O], U8)
+        nc.vector.memset(hq[:], 0)
+        nc.vector.memset(hs[:].bitcast(I32), 0)
+        pages = [[sb_tile("page%d%d" % (s, n), [P, U], F32) for n in range(2)] for s in range(2)]
+        for s in range(2):
+            for n in range(2):
+                nc.vector.memset(pages[s][n][:], 0.0)
+
+        xt_sst = sb_tile("xt_sst", [PACK, QUADS, T // 4], I32)
+        xo_sst = sb_tile("xo_sst", [PACK, QUADS, M // 4], I32)
+        xt_wwin = sb_tile("xt_wwin", [P, T], U32)
+        xo_wwin = sb_tile("xo_wwin", [P, M], U32)
+        w_raw = sb_tile("w_raw", [P, R], U32)
+        w2_raw = sb_tile("w2_raw", [P, R], U16)
+        nc.sync.dma_start(xt_sst[:], by_quadrant(xt_scales))
+        nc.scalar.dma_start(xt_wwin[:].bitcast(I32), words_of(xt_words))
+        nc.sync.dma_start(xo_sst[:], by_quadrant(xo_scales))
+        nc.scalar.dma_start(xo_wwin[:].bitcast(I32), words_of(xo_words))
+        l1 = load_list("l1", offs)
+        nc.scalar.dma_start(w_raw[:].bitcast(I32), words_of(w_words))
+        l2 = load_list("l2", offs2)
+        nc.scalar.dma_start(w2_raw[:].bitcast(I32), w2_words[0].bitcast(I32))
+        nc.gpsimd.dma_start(wsc_stage[0:PACK], by_quadrant(w2_scales))
+        nc.gpsimd.dma_start(wsc_stage[PACK : 2 * PACK], by_quadrant(w_scales))
+        l3 = load_list("l3", offs3)
+        l4 = load_list("l4", offs4)
+        sa_t = sb_tile("sa_t", [P, PACK], F32)
+        sb_t = sb_tile("sb_t", [P, PACK], F32)
+        nc.sync.dma_start(sa_t[:], sa.rearrange("(p t) o -> p (t o)", t=PACK))
+        nc.sync.dma_start(sb_t[:], sb.rearrange("(p t) o -> p (t o)", t=PACK))
+        wb_w = sb_tile("wb_w", [P, 2 * N], U8)
+        wo_w = sb_tile("wo_w", [P, N], U32)
+        nc.sync.dma_start(wo_w[:].bitcast(I32), words_of(wo_words))
+        nc.sync.dma_start(wb_w[:].bitcast(I32), wb_words[0].bitcast(I32))
+        for plane, src in ((wo_sc, wo_scales), (wb_sc, wb_scales)):
+            for q in range(QUADS):
+                nc.sync.dma_start(plane[32 * q : 32 * q + PACK, :].bitcast(I32), src[0, PACK * q : PACK * (q + 1), :].bitcast(I32))
+        l5 = load_list("l5", offs5)
+        l6 = load_list("l6", offs6)
+
+        for stage, win in ((xt_sst, xt_swin), (xo_sst, xo_swin)):
+            for q in range(QUADS):
+                nc.vector.tensor_copy(win[32 * q : 32 * q + PACK, :].bitcast(I32), stage[:, q, :])
+        xt_s = sb_tile("xt_s", [P, J], U8)
+        xo_s = sb_tile("xo_s", [P, J], U8)
+        xt_w = sb_tile("xt_w", [P, J], U32)
+        xo_w = sb_tile("xo_w", [P, J], U32)
+        nc.vector.tensor_copy(xt_s[:], xt_swin[:].indirect(l1[:]))
+        nc.vector.tensor_copy(xt_w[:], xt_wwin[:].indirect(l1[:]))
+        wsc = sb_tile("wsc", [P, R], U8)
+        for q in range(QUADS):
+            nc.vector.tensor_copy(wsc[32 * q : 32 * (q + 1), :].bitcast(I32), wsc_stage[:, q, :])
+        wsc_d = sb_tile("wsc_d", [P, R], U8)
+        nc.vector.tensor_copy(wsc_d[:].rearrange("p (t m) -> p m t", t=PACK), wsc[:].rearrange("p (m t) -> p m t", t=PACK))
+        nc.vector.tensor_copy(xo_s[:], xo_swin[:].indirect(l2[:]))
+        nc.vector.tensor_copy(xo_w[:], xo_wwin[:].indirect(l2[:]))
+        w_d = sb_tile("w_d", [P, R], U32)
+        w2_d = sb_tile("w2_d", [P, R], U16)
+        nc.scalar.copy(w_d[:].rearrange("p (t m) -> p m t", t=PACK), w_raw[:].rearrange("p (m t) -> p m t", t=PACK))
+        nc.scalar.copy(w2_d[:].rearrange("p (t m) -> p m t", t=PACK), w2_raw[:].rearrange("p (m t) -> p m t", t=PACK))
+
+        a_ps = [psum.tile([P, J], F32, name="a_ps%d" % t) for t in range(PACK)]
+        a_sb = [sb_tile("a_sb%d" % t, [P, J], F32) for t in range(PACK)]
+        for t in range(PACK):
+            cols = slice(P * t, P * (t + 1))
+            nc.tensor.matmul_mx(out=a_ps[t][:], lhsT=w_d[:, cols].bitcast(FP8X4), lhsT_scale=wsc_d[PACK:, cols],
+                                rhs=xt_w[:].bitcast(FP8X4), rhs_scale=xt_s[:], start=True, stop=False)
+        for t in range(PACK):
+            cols = slice(P * t, P * (t + 1))
+            nc.tensor.matmul_mx(out=a_ps[t][:], lhsT=w2_d[:, cols].bitcast(U8).bitcast(FP4X4), lhsT_scale=wsc_d[:, cols],
+                                rhs=xo_w[:].bitcast(FP8X4), rhs_scale=xo_s[:], start=False, stop=True)
+            nc.vector.tensor_copy(a_sb[t][:], a_ps[t][:])
+
+        hb = sb_tile("hb", [P, O, PACK], BF16)
+        res = {}
+        for h in range(2):
+            cols = slice(HALF * h, HALF * (h + 1))
+            lcols = slice(HALF // 16 * h, HALF // 16 * (h + 1))
+            diff = sb_tile("diff%d" % h, [P, PACK, HALF], F32)
+            for t in range(PACK):
+                slot = (t + 2 * h) % PACK
+                g = ring.tile([P, 2, HALF], F32, name="g%d%d" % (h, t), tag="g%d" % slot, align_bytes=64)
+                nc.scalar.activation(g[:, 0, :], a_sb[t][:].indirect(l3[:, lcols]), ACT.Copy, scale=sa_t[:, t : t + 1])
+                nc.scalar.activation(g[:, 1, :], a_sb[t][:].indirect(l4[:, lcols]), ACT.Copy, scale=sb_t[:, t : t + 1])
+                nc.vector.tensor_tensor(diff[:, t, :], g[:, 0, :], g[:, 1, :], ALU.subtract)
+            dv = diff[:].rearrange("p t o -> p o t")
+            nc.vector.scalar_tensor_tensor(hb[:, cols, :], dv, -1.0, dv, ALU.mult, ALU.max)
+            nc.vector.quantize_mx(out=hq[:, cols].bitcast(FP8X4), scales=hs[:, cols], in_=hb[:, cols, :].rearrange("p o t -> p (o t)"))
+            for n in range(2):
+                ncols = slice(P * n, P * (n + 1))
+                pq = psum.tile([P, O + HALF], F32, name="pq%d%d" % (h, n))
+                nc.tensor.matmul_mx(out=pq[:, O:], lhsT=wo_w[:, ncols].bitcast(FP8X4), lhsT_scale=wo_sc[:, ncols],
+                                    rhs=hq[:, cols].bitcast(FP8X4), rhs_scale=hs[:, cols], start=True, stop=True)
+                nc.tensor.matmul_mx(out=pq[:, :O], lhsT=wb_w[:, 2 * P * n : 2 * P * (n + 1)].bitcast(FP4X4), lhsT_scale=wb_sc[:, ncols],
+                                    rhs=hq[:].bitcast(FP8X4), rhs_scale=hs[:], start=True, stop=True)
+                r = sb_tile("res%d%d" % (h, n), [P, 2, HALF], F32)
+                src = pq[:].rearrange("p (c o) -> p c o", o=HALF)
+                nc.vector.tensor_copy(r[:], src[:, h :: 2 - h, :])
+                res[h, n] = r
+        for h in range(2):
+            lcols = slice(HALF // 16 * h, HALF // 16 * (h + 1))
+            for n in range(2):
+                nc.scalar.activation(pages[0][n][:].indirect(l5[:, lcols]), res[h, n][:, 0, :], ACT.Copy)
+                nc.scalar.activation(pages[1][n][:].indirect(l6[:, lcols]), res[h, n][:, 1, :], ACT.Copy)
+        for n in range(2):
+            total = sb_tile("total%d" % n, [P, U], F32)
+            nc.vector.tensor_tensor(total[:], pages[0][n][:], pages[1][n][:], ALU.add)
+            nc.sync.dma_start(out[P * n : P * (n + 1), :], total[:])

@@ -46,16 +46,17 @@ def tile_picked_tokens_plain_bank_grouppair_outcomes_twoposted_kernel(
         def words_of(words):
             return words[0].rearrange("p n r -> p (n r)").bitcast(I32)
 
-        wsc_stage = sb_tile("wsc_stage", [32, QUADS, R // 4], I32)
-        nc.vector.memset(wsc_stage[:], 0)
+        wsc_stage = sb_tile("wsc_stage", [2 * PACK, QUADS, R // 4], I32)
+        wsc = sb_tile("wsc", [P, 2, R // 4], I32)
         xt_swin = sb_tile("xt_swin", [P, T], U8)
         xo_swin = sb_tile("xo_swin", [P, M], U8)
-        nc.vector.memset(xt_swin[:].bitcast(I32), 0)
         nc.vector.memset(xo_swin[:].bitcast(I32), 0)
-        wb_sc = sb_tile("wb_sc", [P, N], U8)
-        wo_sc = sb_tile("wo_sc", [P, N], U8)
-        nc.vector.memset(wb_sc[:].bitcast(I32), 0)
-        nc.vector.memset(wo_sc[:].bitcast(I32), 0)
+        nc.vector.memset(xt_swin[:].bitcast(I32), 0)
+        nc.vector.memset(wsc[0:64], 0)
+        osc = sb_tile("osc", [P, 2, N // 4], I32)
+        nc.vector.memset(osc[:], 0)
+        wb_sc = osc[:, 0, :].bitcast(U8)
+        wo_sc = osc[:, 1, :].bitcast(U8)
         hq = sb_tile("hq", [P, O], I32)
         hs = sb_tile("hs", [P, O], U8)
         nc.vector.memset(hq[:], 0)
@@ -63,56 +64,59 @@ def tile_picked_tokens_plain_bank_grouppair_outcomes_twoposted_kernel(
         pages = [[sb_tile("page%d%d" % (s, n), [P, U], F32) for n in range(2)] for s in range(2)]
         for s in range(2):
             for n in range(2):
-                nc.vector.memset(pages[s][n][:], 0.0)
+                nc.gpsimd.memset(pages[s][n][:], 0.0)
 
         xt_sst = sb_tile("xt_sst", [PACK, QUADS, T // 4], I32)
-        xo_sst = sb_tile("xo_sst", [PACK, QUADS, M // 4], I32)
         xt_wwin = sb_tile("xt_wwin", [P, T], U32)
         xo_wwin = sb_tile("xo_wwin", [P, M], U32)
         w_raw = sb_tile("w_raw", [P, R], U32)
         w2_raw = sb_tile("w2_raw", [P, R], U16)
         nc.sync.dma_start(xt_sst[:], by_quadrant(xt_scales))
-        nc.scalar.dma_start(xt_wwin[:].bitcast(I32), words_of(xt_words))
-        nc.sync.dma_start(xo_sst[:], by_quadrant(xo_scales))
-        nc.scalar.dma_start(xo_wwin[:].bitcast(I32), words_of(xo_words))
         l1 = load_list("l1", offs)
-        nc.scalar.dma_start(w_raw[:].bitcast(I32), words_of(w_words))
+        nc.sync.dma_start(xt_wwin[:].bitcast(I32), words_of(xt_words))
+        nc.sync.dma_start(wsc_stage[0:PACK], by_quadrant(w2_scales))
+        nc.sync.dma_start(wsc_stage[PACK : 2 * PACK], by_quadrant(w_scales))
+        nc.sync.dma_start(xo_wwin[:].bitcast(I32), words_of(xo_words))
+        nc.sync.dma_start(w_raw[:].bitcast(I32), words_of(w_words))
         l2 = load_list("l2", offs2)
-        nc.scalar.dma_start(w2_raw[:].bitcast(I32), w2_words[0].bitcast(I32))
-        nc.gpsimd.dma_start(wsc_stage[0:PACK], by_quadrant(w2_scales))
-        nc.gpsimd.dma_start(wsc_stage[PACK : 2 * PACK], by_quadrant(w_scales))
-        l3 = load_list("l3", offs3)
-        l4 = load_list("l4", offs4)
+        for q in range(QUADS):
+            nc.sync.dma_start(xo_swin[32 * q : 32 * q + PACK, :].bitcast(I32), xo_scales[0, PACK * q : PACK * (q + 1), :].bitcast(I32))
+        nc.sync.dma_start(w2_raw[:].bitcast(I32), w2_words[0].bitcast(I32))
         sa_t = sb_tile("sa_t", [P, PACK], F32)
         sb_t = sb_tile("sb_t", [P, PACK], F32)
+        l3 = load_list("l3", offs3)
         nc.sync.dma_start(sa_t[:], sa.rearrange("(p t) o -> p (t o)", t=PACK))
+        l4 = load_list("l4", offs4)
         nc.sync.dma_start(sb_t[:], sb.rearrange("(p t) o -> p (t o)", t=PACK))
         wb_w = sb_tile("wb_w", [P, 2 * N], U8)
         wo_w = sb_tile("wo_w", [P, N], U32)
+        osc_stage = sb_tile("osc_stage", [PACK, 2, QUADS, N // 4], I32)
+        nc.sync.dma_start(osc_stage[:, 0], by_quadrant(wb_scales))
+        nc.sync.dma_start(osc_stage[:, 1], by_quadrant(wo_scales))
         nc.sync.dma_start(wo_w[:].bitcast(I32), words_of(wo_words))
         nc.sync.dma_start(wb_w[:].bitcast(I32), wb_words[0].bitcast(I32))
-        for plane, src in ((wo_sc, wo_scales), (wb_sc, wb_scales)):
-            for q in range(QUADS):
-                nc.sync.dma_start(plane[32 * q : 32 * q + PACK, :].bitcast(I32), src[0, PACK * q : PACK * (q + 1), :].bitcast(I32))
         l5 = load_list("l5", offs5)
         l6 = load_list("l6", offs6)
 
-        for stage, win in ((xt_sst, xt_swin), (xo_sst, xo_swin)):
+        def spread(win, stage):
             for q in range(QUADS):
                 nc.vector.tensor_copy(win[32 * q : 32 * q + PACK, :].bitcast(I32), stage[:, q, :])
+
+        spread(xt_swin, xt_sst)
         xt_s = sb_tile("xt_s", [P, J], U8)
         xo_s = sb_tile("xo_s", [P, J], U8)
         xt_w = sb_tile("xt_w", [P, J], U32)
         xo_w = sb_tile("xo_w", [P, J], U32)
         nc.vector.tensor_copy(xt_s[:], xt_swin[:].indirect(l1[:]))
         nc.vector.tensor_copy(xt_w[:], xt_wwin[:].indirect(l1[:]))
-        wsc = sb_tile("wsc", [P, R], U8)
-        for q in range(QUADS):
-            nc.vector.tensor_copy(wsc[32 * q : 32 * (q + 1), :].bitcast(I32), wsc_stage[:, q, :])
+        nc.vector.tensor_copy(wsc[0 : 2 * PACK], wsc_stage[:, 0::2, :])
+        for h in range(2):
+            nc.vector.tensor_copy(wsc[32 : 32 + 2 * PACK, h, :], wsc_stage[:, 2 * h + 1, :])
+        nc.vector.tensor_copy(wsc[64:128, 0, :], wsc[0:64, 1, :])
         wsc_d = sb_tile("wsc_d", [P, R], U8)
-        nc.vector.tensor_copy(wsc_d[:].rearrange("p (t m) -> p m t", t=PACK), wsc[:].rearrange("p (m t) -> p m t", t=PACK))
-        nc.vector.tensor_copy(xo_s[:], xo_swin[:].indirect(l2[:]))
+        nc.vector.tensor_copy(wsc_d[:].rearrange("p (t m) -> p m t", t=PACK), wsc[:, 0, :].bitcast(U8).rearrange("p (m t) -> p m t", t=PACK))
         nc.vector.tensor_copy(xo_w[:], xo_wwin[:].indirect(l2[:]))
+        nc.vector.tensor_copy(xo_s[:], xo_swin[:].indirect(l2[:]))
         w_d = sb_tile("w_d", [P, R], U32)
         w2_d = sb_tile("w2_d", [P, R], U16)
         nc.scalar.copy(w_d[:].rearrange("p (t m) -> p m t", t=PACK), w_raw[:].rearrange("p (m t) -> p m t", t=PACK))
@@ -130,21 +134,27 @@ def tile_picked_tokens_plain_bank_grouppair_outcomes_twoposted_kernel(
                                 rhs=xo_w[:].bitcast(FP8X4), rhs_scale=xo_s[:], start=False, stop=True)
             nc.vector.tensor_copy(a_sb[t][:], a_ps[t][:])
 
-        hb = sb_tile("hb", [P, O, PACK], BF16)
+        for q in range(QUADS):
+            nc.vector.tensor_copy(osc[32 * q : 32 * q + PACK], osc_stage[:, :, q, :])
         res = {}
         for h in range(2):
             cols = slice(HALF * h, HALF * (h + 1))
             lcols = slice(HALF // 16 * h, HALF // 16 * (h + 1))
-            diff = sb_tile("diff%d" % h, [P, PACK, HALF], F32)
+            diff = ring.tile([P, 2, PACK, HALF], F32, name="diff%d" % h, tag="hold%d" % h, align_bytes=64)
             for t in range(PACK):
                 slot = (t + 2 * h) % PACK
                 g = ring.tile([P, 2, HALF], F32, name="g%d%d" % (h, t), tag="g%d" % slot, align_bytes=64)
                 nc.scalar.activation(g[:, 0, :], a_sb[t][:].indirect(l3[:, lcols]), ACT.Copy, scale=sa_t[:, t : t + 1])
                 nc.scalar.activation(g[:, 1, :], a_sb[t][:].indirect(l4[:, lcols]), ACT.Copy, scale=sb_t[:, t : t + 1])
-                nc.vector.tensor_tensor(diff[:, t, :], g[:, 0, :], g[:, 1, :], ALU.subtract)
-            dv = diff[:].rearrange("p t o -> p o t")
-            nc.vector.scalar_tensor_tensor(hb[:, cols, :], dv, -1.0, dv, ALU.mult, ALU.max)
-            nc.vector.quantize_mx(out=hq[:, cols].bitcast(FP8X4), scales=hs[:, cols], in_=hb[:, cols, :].rearrange("p o t -> p (o t)"))
+                nc.vector.tensor_tensor(diff[:, :, t, :], g[:], g[:, ::-1, :], ALU.subtract)
+            hb = ring.tile([P, HALF, PACK], BF16, name="hb%d" % h, tag="hold%d" % (h + 1), align_bytes=64)
+            nc.vector.tensor_tensor(
+                hb[:].rearrange("p (c i) t -> p c t i", i=4),
+                diff[:, 0].rearrange("p t (c i) -> p c t i", i=4),
+                diff[:, 1].rearrange("p t (c i) -> p c t i", i=4),
+                ALU.max,
+            )
+            nc.vector.quantize_mx(out=hq[:, cols].bitcast(FP8X4), scales=hs[:, cols], in_=hb[:].rearrange("p o t -> p (o t)"))
             for n in range(2):
                 ncols = slice(P * n, P * (n + 1))
                 pq = psum.tile([P, O + HALF], F32, name="pq%d%d" % (h, n))

@@ -46,6 +46,8 @@ def tile_picked_tokens_plain_bank_grouppair_outcomes_twoposted_kernel(
         def words_of(words):
             return words[0].rearrange("p n r -> p (n r)").bitcast(I32)
 
+        sa_t = sb_tile("sa_t", [P, PACK], F32)
+        sb_t = sb_tile("sb_t", [P, PACK], F32)
         wsc_stage = sb_tile("wsc_stage", [2 * PACK, QUADS, R // 4], I32)
         wsc = sb_tile("wsc", [P, 2, R // 4], I32)
         xt_swin = sb_tile("xt_swin", [P, T], U8)
@@ -59,12 +61,12 @@ def tile_picked_tokens_plain_bank_grouppair_outcomes_twoposted_kernel(
         wo_sc = osc[:, 1, :].bitcast(U8)
         hq = sb_tile("hq", [P, O], I32)
         hs = sb_tile("hs", [P, O], U8)
-        nc.vector.memset(hq[:], 0)
-        nc.vector.memset(hs[:].bitcast(I32), 0)
+        nc.vector.memset(hq[:, HALF:], 0)
+        nc.vector.memset(hs[:, HALF:].bitcast(I32), 0)
         pages = [[sb_tile("page%d%d" % (s, n), [P, U], F32) for n in range(2)] for s in range(2)]
         for s in range(2):
             for n in range(2):
-                nc.gpsimd.memset(pages[s][n][:], 0.0)
+                nc.vector.memset(pages[s][n][:], 0.0)
 
         xt_sst = sb_tile("xt_sst", [PACK, QUADS, T // 4], I32)
         xt_wwin = sb_tile("xt_wwin", [P, T], U32)
@@ -76,14 +78,12 @@ def tile_picked_tokens_plain_bank_grouppair_outcomes_twoposted_kernel(
         nc.sync.dma_start(xt_wwin[:].bitcast(I32), words_of(xt_words))
         nc.sync.dma_start(wsc_stage[0:PACK], by_quadrant(w2_scales))
         nc.sync.dma_start(wsc_stage[PACK : 2 * PACK], by_quadrant(w_scales))
-        nc.sync.dma_start(xo_wwin[:].bitcast(I32), words_of(xo_words))
-        nc.sync.dma_start(w_raw[:].bitcast(I32), words_of(w_words))
         l2 = load_list("l2", offs2)
+        nc.sync.dma_start(w_raw[:].bitcast(I32), words_of(w_words))
+        nc.sync.dma_start(xo_wwin[:].bitcast(I32), words_of(xo_words))
         for q in range(QUADS):
             nc.sync.dma_start(xo_swin[32 * q : 32 * q + PACK, :].bitcast(I32), xo_scales[0, PACK * q : PACK * (q + 1), :].bitcast(I32))
         nc.sync.dma_start(w2_raw[:].bitcast(I32), w2_words[0].bitcast(I32))
-        sa_t = sb_tile("sa_t", [P, PACK], F32)
-        sb_t = sb_tile("sb_t", [P, PACK], F32)
         l3 = load_list("l3", offs3)
         nc.sync.dma_start(sa_t[:], sa.rearrange("(p t) o -> p (t o)", t=PACK))
         l4 = load_list("l4", offs4)
@@ -114,15 +114,18 @@ def tile_picked_tokens_plain_bank_grouppair_outcomes_twoposted_kernel(
             nc.vector.tensor_copy(wsc[32 : 32 + 2 * PACK, h, :], wsc_stage[:, 2 * h + 1, :])
         nc.vector.tensor_copy(wsc[64:128, 0, :], wsc[0:64, 1, :])
         wsc_d = sb_tile("wsc_d", [P, R], U8)
-        nc.vector.tensor_copy(wsc_d[:].rearrange("p (t m) -> p m t", t=PACK), wsc[:, 0, :].bitcast(U8).rearrange("p (m t) -> p m t", t=PACK))
+        nc.vector.tensor_copy(wsc_d[:].rearrange("p (t m) -> p t m", t=PACK), wsc[:, 0, :].bitcast(U8).rearrange("p (m t) -> p t m", t=PACK))
         nc.vector.tensor_copy(xo_w[:], xo_wwin[:].indirect(l2[:]))
         nc.vector.tensor_copy(xo_s[:], xo_swin[:].indirect(l2[:]))
         w_d = sb_tile("w_d", [P, R], U32)
         w2_d = sb_tile("w2_d", [P, R], U16)
-        nc.scalar.copy(w_d[:].rearrange("p (t m) -> p m t", t=PACK), w_raw[:].rearrange("p (m t) -> p m t", t=PACK))
-        nc.scalar.copy(w2_d[:].rearrange("p (t m) -> p m t", t=PACK), w2_raw[:].rearrange("p (m t) -> p m t", t=PACK))
+        for u in range(2):
+            pair = slice(2 * u, 2 * u + 2)
+            nc.scalar.copy(w_d[:].rearrange("p (t m) -> p m t", t=PACK)[:, :, pair], w_raw[:].rearrange("p (m t) -> p m t", t=PACK)[:, :, pair])
+        for t in range(PACK):
+            nc.scalar.copy(w2_d[:, P * t : P * (t + 1)], w2_raw[:, t::PACK])
 
-        a_ps = [psum.tile([P, J], F32, name="a_ps%d" % t) for t in range(PACK)]
+        a_ps = [psum.tile([P, J], F32, name="a_ps%d" % t, tag="a_ps%d" % t) for t in range(PACK)]
         a_sb = [sb_tile("a_sb%d" % t, [P, J], F32) for t in range(PACK)]
         for t in range(PACK):
             cols = slice(P * t, P * (t + 1))
@@ -155,22 +158,25 @@ def tile_picked_tokens_plain_bank_grouppair_outcomes_twoposted_kernel(
                 ALU.max,
             )
             nc.vector.quantize_mx(out=hq[:, cols].bitcast(FP8X4), scales=hs[:, cols], in_=hb[:].rearrange("p o t -> p (o t)"))
-            for n in range(2):
+            r = sb_tile("res%d" % h, [P, 4, HALF], F32)
+            first = psum.tile([P, HALF], F32, name="first%d" % h)
+            second = psum.tile([P, O], F32, name="second%d" % h)
+            rest = psum.tile([P, O + HALF], F32, name="rest%d" % h, tag="a_ps%d" % h)
+            for n, (q_ps, p_ps) in enumerate(((first[:], second[:]), (rest[:, O:], rest[:, :O]))):
                 ncols = slice(P * n, P * (n + 1))
-                pq = psum.tile([P, O + HALF], F32, name="pq%d%d" % (h, n))
-                nc.tensor.matmul_mx(out=pq[:, O:], lhsT=wo_w[:, ncols].bitcast(FP8X4), lhsT_scale=wo_sc[:, ncols],
+                nc.tensor.matmul_mx(out=q_ps, lhsT=wo_w[:, ncols].bitcast(FP8X4), lhsT_scale=wo_sc[:, ncols],
                                     rhs=hq[:, cols].bitcast(FP8X4), rhs_scale=hs[:, cols], start=True, stop=True)
-                nc.tensor.matmul_mx(out=pq[:, :O], lhsT=wb_w[:, 2 * P * n : 2 * P * (n + 1)].bitcast(FP4X4), lhsT_scale=wb_sc[:, ncols],
+                nc.tensor.matmul_mx(out=p_ps, lhsT=wb_w[:, 2 * P * n : 2 * P * (n + 1)].bitcast(FP4X4), lhsT_scale=wb_sc[:, ncols],
                                     rhs=hq[:].bitcast(FP8X4), rhs_scale=hs[:], start=True, stop=True)
-                r = sb_tile("res%d%d" % (h, n), [P, 2, HALF], F32)
-                src = pq[:].rearrange("p (c o) -> p c o", o=HALF)
-                nc.vector.tensor_copy(r[:], src[:, h :: 2 - h, :])
-                res[h, n] = r
+            nc.vector.tensor_copy(r[:, 1, :], first[:])
+            nc.vector.tensor_copy(r[:, 0, :], second[:, cols])
+            nc.vector.tensor_copy(r[:, 2:, :], rest[:].rearrange("p (c o) -> p c o", o=HALF)[:, h :: 2 - h, :])
+            res[h] = r
         for h in range(2):
             lcols = slice(HALF // 16 * h, HALF // 16 * (h + 1))
             for n in range(2):
-                nc.scalar.activation(pages[0][n][:].indirect(l5[:, lcols]), res[h, n][:, 0, :], ACT.Copy)
-                nc.scalar.activation(pages[1][n][:].indirect(l6[:, lcols]), res[h, n][:, 1, :], ACT.Copy)
+                nc.scalar.activation(pages[1][n][:].indirect(l6[:, lcols]), res[h][:, 2 * n + 1, :], ACT.Copy)
+                nc.scalar.activation(pages[0][n][:].indirect(l5[:, lcols]), res[h][:, 2 * n, :], ACT.Copy)
         for n in range(2):
             total = sb_tile("total%d" % n, [P, U], F32)
             nc.vector.tensor_tensor(total[:], pages[0][n][:], pages[1][n][:], ALU.add)

from contextlib import ExitStack

import concourse.mybir as mybir

F32 = mybir.dt.float32
BF16 = mybir.dt.bfloat16
I32 = mybir.dt.int32
U32 = mybir.dt.uint32
U16 = mybir.dt.uint16
U8 = mybir.dt.uint8
FP8X4 = mybir.dt.float8_e4m3fn_x4
FP4X4 = mybir.dt.float4_e2m1fn_x4
ACT = mybir.ActivationFunctionType
ALU = mybir.AluOpType

P = 128
K, J, R, T, Z, M, O, N, U = 512, 256, 512, 1024, 512, 1024, 128, 256, 256
PACK = 4
QUADS = 4
HALF = O // 2
FLOPS = 2 * (K * R * J + Z * R * J + 2 * R * N * O)


def tile_picked_tokens_plain_bank_grouppair_outcomes_twoposted_kernel(
    tc, xt_words, xt_scales, w_words, w_scales, xo_words, xo_scales, w2_words, w2_scales, sa, sb,
    wb_words, wb_scales, wo_words, wo_scales, offs, offs2, offs3, offs4, offs5, offs6, out,
):
    nc = tc.nc
    with ExitStack() as ctx:
        lists = ctx.enter_context(tc.tile_pool(name="lists", bufs=1))
        keep = ctx.enter_context(tc.tile_pool(name="keep", bufs=1))
        ring = ctx.enter_context(tc.tile_pool(name="ring", bufs=1))
        psum = ctx.enter_context(tc.psum_pool(name="psum", bufs=1))

        def sb_tile(name, shape, dtype):
            return keep.tile(shape, dtype, name=name, align_bytes=64)

        def load_list(name, src):
            t = lists.tile(list(src.shape), U16, name=name)
            nc.sync.dma_start(t[:], src)
            return t

        def by_quadrant(scales):
            return scales[0].rearrange("(q i) n -> i q n", i=PACK).bitcast(I32)

        def words_of(words):
            return words[0].rearrange("p n r -> p (n r)").bitcast(I32)

        sa_t = sb_tile("sa_t", [P, PACK], F32)
        sb_t = sb_tile("sb_t", [P, PACK], F32)
        wsc_stage = sb_tile("wsc_stage", [2 * PACK, QUADS, R // 4], I32)
        wsc = sb_tile("wsc", [P, 2, R // 4], I32)
        xt_swin = sb_tile("xt_swin", [P, T], U8)
        xo_swin = sb_tile("xo_swin", [P, M], U8)
        nc.vector.memset(xo_swin[:].bitcast(I32), 0)
        nc.vector.memset(xt_swin[:].bitcast(I32), 0)
        nc.vector.memset(wsc[0:64], 0)
        osc = sb_tile("osc", [P, 2, N // 4], I32)
        nc.vector.memset(osc[:], 0)
        wb_sc = osc[:, 0, :].bitcast(U8)
        wo_sc = osc[:, 1, :].bitcast(U8)
        hq = sb_tile("hq", [P, O], I32)
        hs = sb_tile("hs", [P, O], U8)
        nc.vector.memset(hq[:, HALF:], 0)
        nc.vector.memset(hs[:, HALF:].bitcast(I32), 0)
        pages = [[sb_tile("page%d%d" % (s, n), [P, U], F32) for n in range(2)] for s in range(2)]
        for s in range(2):
            for n in range(2):
                nc.vector.memset(pages[s][n][:], 0.0)

        xt_sst = sb_tile("xt_sst", [PACK, QUADS, T // 4], I32)
        xt_wwin = sb_tile("xt_wwin", [P, T], U32)
        xo_wwin = sb_tile("xo_wwin", [P, M], U32)
        w_raw = sb_tile("w_raw", [P, R], U32)
        w2_raw = sb_tile("w2_raw", [P, R], U16)
        nc.sync.dma_start(xt_sst[:], by_quadrant(xt_scales))
        l1 = load_list("l1", offs)
        nc.sync.dma_start(xt_wwin[:].bitcast(I32), words_of(xt_words))
        nc.sync.dma_start(wsc_stage[0:PACK], by_quadrant(w2_scales))
        nc.sync.dma_start(wsc_stage[PACK : 2 * PACK], by_quadrant(w_scales))
        l2 = load_list("l2", offs2)
        nc.sync.dma_start(w_raw[:].bitcast(I32), words_of(w_words))
        nc.sync.dma_start(xo_wwin[:].bitcast(I32), words_of(xo_words))
        for q in range(QUADS):
            nc.sync.dma_start(xo_swin[32 * q : 32 * q + PACK, :].bitcast(I32), xo_scales[0, PACK * q : PACK * (q + 1), :].bitcast(I32))
        nc.sync.dma_start(w2_raw[:].bitcast(I32), w2_words[0].bitcast(I32))
        l3 = load_list("l3", offs3)
        nc.sync.dma_start(sa_t[:], sa.rearrange("(p t) o -> p (t o)", t=PACK))
        l4 = load_list("l4", offs4)
        nc.sync.dma_start(sb_t[:], sb.rearrange("(p t) o -> p (t o)", t=PACK))
        wb_w = sb_tile("wb_w", [P, 2 * N], U8)
        wo_w = sb_tile("wo_w", [P, N], U32)
        osc_stage = sb_tile("osc_stage", [PACK, 2, QUADS, N // 4], I32)
        nc.sync.dma_start(osc_stage[:, 0], by_quadrant(wb_scales))
        nc.sync.dma_start(osc_stage[:, 1], by_quadrant(wo_scales))
        nc.sync.dma_start(wo_w[:].bitcast(I32), words_of(wo_words))
        nc.sync.dma_start(wb_w[:].bitcast(I32), wb_words[0].bitcast(I32))
        l5 = load_list("l5", offs5)
        l6 = load_list("l6", offs6)

        def spread(win, stage):
            for q in range(QUADS):
                nc.vector.tensor_copy(win[32 * q : 32 * q + PACK, :].bitcast(I32), stage[:, q, :])

        spread(xt_swin, xt_sst)
        xt_s = sb_tile("xt_s", [P, J], U8)
        xo_s = sb_tile("xo_s", [P, J], U8)
        xt_w = sb_tile("xt_w", [P, J], U32)
        xo_w = sb_tile("xo_w", [P, J], U32)
        nc.vector.tensor_copy(xt_s[:], xt_swin[:].indirect(l1[:]))
        nc.vector.tensor_copy(xt_w[:], xt_wwin[:].indirect(l1[:]))
        nc.vector.tensor_copy(wsc[0 : 2 * PACK], wsc_stage[:, 0::2, :])
        for h in range(2):
            nc.vector.tensor_copy(wsc[32 : 32 + 2 * PACK, h, :], wsc_stage[:, 2 * h + 1, :])
        nc.vector.tensor_copy(wsc[64:128, 0, :], wsc[0:64, 1, :])
        wsc_d = sb_tile("wsc_d", [P, R], U8)
        nc.vector.tensor_copy(wsc_d[:].rearrange("p (t m) -> p t m", t=PACK), wsc[:, 0, :].bitcast(U8).rearrange("p (m t) -> p t m", t=PACK))
        nc.vector.tensor_copy(xo_w[:], xo_wwin[:].indirect(l2[:]))
        nc.vector.tensor_copy(xo_s[:], xo_swin[:].indirect(l2[:]))
        w_d = sb_tile("w_d", [P, R], U32)
        w2_d = sb_tile("w2_d", [P, R], U16)
        for u in range(2):
            pair = slice(2 * u, 2 * u + 2)
            nc.scalar.copy(w_d[:].rearrange("p (t m) -> p m t", t=PACK)[:, :, pair], w_raw[:].rearrange("p (m t) -> p m t", t=PACK)[:, :, pair])
        for t in range(PACK):
            nc.scalar.copy(w2_d[:, P * t : P * (t + 1)], w2_raw[:, t::PACK])

        a_ps = [psum.tile([P, J], F32, name="a_ps%d" % t, tag="a_ps%d" % t) for t in range(PACK)]
        a_sb = [sb_tile("a_sb%d" % t, [P, J], F32) for t in range(PACK)]
        for t in range(PACK):
            cols = slice(P * t, P * (t + 1))
            nc.tensor.matmul_mx(out=a_ps[t][:], lhsT=w_d[:, cols].bitcast(FP8X4), lhsT_scale=wsc_d[PACK:, cols],
                                rhs=xt_w[:].bitcast(FP8X4), rhs_scale=xt_s[:], start=True, stop=False)
        for t in range(PACK):
            cols = slice(P * t, P * (t + 1))
            nc.tensor.matmul_mx(out=a_ps[t][:], lhsT=w2_d[:, cols].bitcast(U8).bitcast(FP4X4), lhsT_scale=wsc_d[:, cols],
                                rhs=xo_w[:].bitcast(FP8X4), rhs_scale=xo_s[:], start=False, stop=True)
            nc.vector.tensor_copy(a_sb[t][:], a_ps[t][:])

        for q in range(QUADS):
            nc.vector.tensor_copy(osc[32 * q : 32 * q + PACK], osc_stage[:, :, q, :])
        res = {}
        for h in range(2):
            cols = slice(HALF * h, HALF * (h + 1))
            lcols = slice(HALF // 16 * h, HALF // 16 * (h + 1))
            diff = ring.tile([P, 2, PACK, HALF], F32, name="diff%d" % h, tag="hold%d" % h, align_bytes=64)
            for t in range(PACK):
                slot = (t + 2 * h) % PACK
                g = ring.tile([P, 2, HALF], F32, name="g%d%d" % (h, t), tag="g%d" % slot, align_bytes=64)
                nc.scalar.activation(g[:, 0, :], a_sb[t][:].indirect(l3[:, lcols]), ACT.Copy, scale=sa_t[:, t : t + 1])
                nc.scalar.activation(g[:, 1, :], a_sb[t][:].indirect(l4[:, lcols]), ACT.Copy, scale=sb_t[:, t : t + 1])
                nc.vector.tensor_tensor(diff[:, :, t, :], g[:], g[:, ::-1, :], ALU.subtract)
            hb = ring.tile([P, HALF, PACK], BF16, name="hb%d" % h, tag="hold%d" % (h + 1), align_bytes=64)
            nc.vector.tensor_tensor(
                hb[:].rearrange("p (c i) t -> p c t i", i=4),
                diff[:, 0].rearrange("p t (c i) -> p c t i", i=4),
                diff[:, 1].rearrange("p t (c i) -> p c t i", i=4),
                ALU.max,
            )
            nc.vector.quantize_mx(out=hq[:, cols].bitcast(FP8X4), scales=hs[:, cols], in_=hb[:].rearrange("p o t -> p (o t)"))
            r = sb_tile("res%d" % h, [P, 4, HALF], F32)
            first = psum.tile([P, HALF], F32, name="first%d" % h)
            second = psum.tile([P, O], F32, name="second%d" % h)
            rest = psum.tile([P, O + HALF], F32, name="rest%d" % h, tag="a_ps%d" % h)
            for n, (q_ps, p_ps) in enumerate(((first[:], second[:]), (rest[:, O:], rest[:, :O]))):
                ncols = slice(P * n, P * (n + 1))
                nc.tensor.matmul_mx(out=q_ps, lhsT=wo_w[:, ncols].bitcast(FP8X4), lhsT_scale=wo_sc[:, ncols],
                                    rhs=hq[:, cols].bitcast(FP8X4), rhs_scale=hs[:, cols], start=True, stop=True)
                nc.tensor.matmul_mx(out=p_ps, lhsT=wb_w[:, 2 * P * n : 2 * P * (n + 1)].bitcast(FP4X4), lhsT_scale=wb_sc[:, ncols],
                                    rhs=hq[:].bitcast(FP8X4), rhs_scale=hs[:], start=True, stop=True)
            nc.vector.tensor_copy(r[:, 1, :], first[:])
            nc.vector.tensor_copy(r[:, 0, :], second[:, cols])
            nc.vector.tensor_copy(r[:, 2:, :], rest[:].rearrange("p (c o) -> p c o", o=HALF)[:, h :: 2 - h, :])
            res[h] = r
        for h in range(2):
            lcols = slice(HALF // 16 * h, HALF // 16 * (h + 1))
            for n in range(2):
                nc.scalar.activation(pages[1][n][:].indirect(l6[:, lcols]), res[h][:, 2 * n + 1, :], ACT.Copy)
                nc.scalar.activation(pages[0][n][:].indirect(l5[:, lcols]), res[h][:, 2 * n, :], ACT.Copy)
        for n in range(2):
            total = sb_tile("total%d" % n, [P, U], F32)
            nc.vector.tensor_tensor(total[:], pages[0][n][:], pages[1][n][:], ALU.add)
            nc.sync.dma_start(out[P * n : P * (n + 1), :], total[:])
